import numpy as np, ml_dtypes
CORES = [3,5,19,21,35,37,51,53,67,69]
N = 10
import mx_ref
NC, G = 128, 4
C = np.float32(0.0259)
BF = ml_dtypes.bfloat16
def cut(t, i, w=512):
    return t[:, w * i:w * i + w]
def tile(rs):
    return np.stack(rs, axis=2).reshape(128, -1).astype(BF)
def layer(w, X):
    out = []
    for i in range(G):
        for t in range(len(X)):
            p = mx_ref.matmul(mx_ref.quantize(cut(w, len(X) * i + t)), X[t])
            z = p if t == 0 else z + p
        out.append(z)
    return out
def act(Z):
    return [np.maximum(z, 0) * C for z in Z]
def setup_inputs(rng):
    def f(*shape):
        return mx_ref.flush((rng.standard_normal(shape, dtype=np.float32) * np.exp2(rng.integers(-2, 3, shape[:-1] + (1,)))).astype(BF))
    return {"s": f(N, 128, 4 * NC), "x": f(N, 128, 4 * NC), "w": f(N, 128, 2 * G * 512), "v": f(N, 128, 512)}
def setup_inputs_blocks(rng):
    d = setup_inputs(rng)
    for k in ("s", "x", "v"): d[k] = mx_ref.spread(d[k], rng, 4)
    for k in ("w",): d[k] = mx_ref.spread(d[k], rng, 1)
    return d
def setup_inputs_wide(rng):
    d = setup_inputs(rng)
    for k in ("s", "x", "v"): d[k] = mx_ref.flush((d[k].astype(np.float32) * np.exp2(rng.integers(-6, 7, (N, 1, 1))).astype(np.float32)).astype(BF))
    return d
def setup_inputs_zeros(rng):
    d = setup_inputs(rng); v = d["x"].reshape(N, 128, -1, 4).copy()
    v[np.broadcast_to((rng.random((N, 1, v.shape[2], 1)) < 0.33), v.shape)] = 0
    d["x"] = v.reshape(d["x"].shape)
    return d
def reference(s, x, w, v):
    q = mx_ref.quantize(s[0])
    y = np.zeros((N, 128, NC), np.float32)
    for r in range(N):
        q = mx_ref.quantize(tile(act(layer(w[r], [q, mx_ref.quantize(x[r])]))))
        y[r] = mx_ref.matmul(mx_ref.quantize(v[r]), q)
    return {"y": y}

@@ -1,0 +1,147 @@
+from concourse.mybir import dt, AluOpType, ActivationFunctionType
+
+NC = 128
+TW = 4 * NC
+G = 4
+C = 0.0259
+BANK = 512
+PIECES = ((0, 4), (4, 7), (7, 8))
+SEND_ENGINES = 8
+
+SCRATCH = {
+    "sb": ("sbuf", [128, TW], "bfloat16"),
+    "xb": ("sbuf", [128, TW], "bfloat16"),
+    "wb": ("sbuf", [128, 2 * G * TW], "bfloat16"),
+    "vb": ("sbuf", [128, TW], "bfloat16"),
+    "h": ("sbuf", [128, TW], "bfloat16"),
+    "cqi": ("sbuf", [128, NC], "float8_e4m3fn_x4"), "pqi": ("sbuf", [128, NC], "uint8"),
+    "cx": ("sbuf", [128, NC], "float8_e4m3fn_x4"), "px": ("sbuf", [128, NC], "uint8"),
+    "cw": ("sbuf", [128, 2 * G * NC], "float8_e4m3fn_x4"), "pw": ("sbuf", [128, 2 * G * NC], "uint8"),
+    "cv": ("sbuf", [128, NC], "float8_e4m3fn_x4"), "pv": ("sbuf", [128, NC], "uint8"),
+    "cqo": ("sbuf", [128, NC], "float8_e4m3fn_x4"), "pqo": ("sbuf", [128, NC], "uint8"),
+    "ysb": ("sbuf", [128, NC], "float32"),
+    "z": ("psum", [128, G * BANK], "float32"),
+    "yp": ("psum", [128, BANK], "float32"),
+}
+SEMAPHORES = (["ls", "lx", "lv", "lw0", "lw1", "lw2"]
+              + ["qs", "qx", "qv", "qw0", "qw1", "qw2", "qo"]
+              + ["mm0", "mm1", "mm2", "mm3", "acts", "ymm", "ycp", "yst"]
+              + ["arrived", "sent"])
+
+
+def hop_mask(topo, src, dst):
+    allowed = topo.mask(src, dst)
+    engines = [e for e in range(allowed.bit_length()) if (allowed >> e) & 1]
+    chosen = engines[::max(1, len(engines) // SEND_ENGINES)]
+    return sum(1 << e for e in chosen), len(chosen)
+
+
+def rank_program(g, core, T, topo):
+    rank = T.rank_of(core)
+    if rank is None:
+        return
+    n_ranks = len(T.cores)
+    first, last = rank == 0, rank == n_ranks - 1
+    sem = T.sem
+    TE, V, S, SY = g.tensor, g.vector, g.scalar, g.sync
+    if not last:
+        nxt = T.cores[rank + 1]
+        if not topo.may_write(core, nxt):
+            raise ValueError("no direct write from core %d to core %d" % (core, nxt))
+        out_mask, out_engines = hop_mask(topo, core, nxt)
+
+    if first:
+        SY.dma_start(T.sb[:], T.s[:]).then_inc(sem.ls, 16)
+    S.dma_start(T.xb[:], T.x[:]).then_inc(sem.lx, 16)
+    for j, (a, b) in enumerate(PIECES):
+        (S if j % 2 else SY).dma_start(T.wb[:, TW * a:TW * b], T.w[:, TW * a:TW * b]).then_inc(sem["lw%d" % j], 16)
+    if first:
+        SY.wait_ge(sem.sent, 2 * out_engines)
+        SY.dma_start(T.vb[:], T.v[:]).then_inc(sem.lv, 16)
+    else:
+        S.dma_start(T.vb[:], T.v[:]).then_inc(sem.lv, 16)
+
+    def quantise(loaded, codes, plane, tile, done):
+        V.wait_ge(loaded, 16)
+        V.quantize_mx(codes, plane, tile).then_inc(done, 1)
+
+    def quantise_w(j):
+        a, b = PIECES[j]
+        quantise(sem["lw%d" % j], T.cw[:, NC * a:NC * b], T.pw[:, NC * a:NC * b], T.wb[:, TW * a:TW * b], sem["qw%d" % j])
+
+    def product(i, t, start, stop):
+        k = 2 * i + t
+        rhs, rhs_scale = (T.cqi, T.pqi) if t == 0 else (T.cx, T.px)
+        return TE.matmul_mx(T.z[:, BANK * i:BANK * i + NC], T.cw[:, NC * k:NC * k + NC], T.pw[:, NC * k:NC * k + NC],
+                            rhs[:], rhs_scale[:], start, stop)
+
+    def act(b):
+        out, z = T.h[:, b:TW:G], T.z[:, BANK * b:BANK * b + NC]
+        if b % 2:
+            V.wait_ge(sem["mm%d" % b], 1)
+            V.tensor_scalar(out, z, 0.0, C, AluOpType.max, AluOpType.mult).then_inc(sem.acts, 1)
+        else:
+            S.wait_ge(sem["mm%d" % b], 1)
+            S.activation(out, z, ActivationFunctionType.Relu, scale=C).then_inc(sem.acts, 1)
+
+    piece_of = {k: j for j, (a, b) in enumerate(PIECES) for k in range(a, b)}
+    if first:
+        quantise(sem.ls, T.cqi[:], T.pqi[:], T.sb[:], sem.qs)
+        quantise(sem.lx, T.cx[:], T.px[:], T.xb[:], sem.qx)
+        quantise_w(0)
+        act(1)
+        quantise_w(1)
+        quantise_w(2)
+        TE.wait_ge(sem.qs, 1)
+        TE.wait_ge(sem.qx, 1)
+        seen = -1
+        for i in range(G):
+            for t in range(2):
+                if piece_of[2 * i + t] > seen:
+                    seen = piece_of[2 * i + t]
+                    TE.wait_ge(sem["qw%d" % seen], 1)
+                p = product(i, t, t == 0, t == 1)
+            p.then_inc(sem["mm%d" % i], 1)
+        act(0)
+        act(2)
+        act(3)
+    else:
+        quantise(sem.lx, T.cx[:], T.px[:], T.xb[:], sem.qx)
+        for j in range(len(PIECES)):
+            quantise_w(j)
+        quantise(sem.lv, T.cv[:], T.pv[:], T.vb[:], sem.qv)
+        TE.wait_ge(sem.qx, 1)
+        seen = -1
+        for i in range(G):
+            if piece_of[2 * i + 1] > seen:
+                for j in range(seen + 1, piece_of[2 * i + 1] + 1):
+                    TE.wait_ge(sem["qw%d" % j], 1)
+                seen = piece_of[2 * i + 1]
+            product(i, 1, True, False)
+        in_engines = hop_mask(topo, T.cores[rank - 1], core)[1]
+        TE.wait_ge(sem.arrived, 2 * in_engines)
+        for i in range(G):
+            product(i, 0, False, True).then_inc(sem["mm%d" % i], 1)
+            act(i)
+
+    V.wait_ge(sem.acts, G)
+    V.quantize_mx(T.cqo[:], T.pqo[:], T.h[:]).then_inc(sem.qo, 1)
+    if not last:
+        rid, pid, _ = topo.addr(nxt)
+        g.wait_ge(sem.qo, 1)
+        g.remote_dma(T.cqi[:].bitcast(dt.uint8), T.cqo[:].bitcast(dt.uint8), sem.arrived, sem.sent, pid, rid, out_mask)
+        g.remote_dma(T.pqi[:], T.pqo[:], sem.arrived, sem.sent, pid, rid, out_mask)
+        g.wait_ge(sem.sent, 2 * out_engines)
+
+    if first:
+        quantise(sem.lv, T.cv[:], T.pv[:], T.vb[:], sem.qv)
+    TE.wait_ge(sem.qv, 1)
+    TE.wait_ge(sem.qo, 1)
+    TE.matmul_mx(T.yp[:, 0:NC], T.cv[:], T.pv[:], T.cqo[:], T.pqo[:], True, True).then_inc(sem.ymm, 1)
+    V.wait_ge(sem.ymm, 1)
+    V.tensor_copy(T.ysb[:], T.yp[:, 0:NC]).then_inc(sem.ycp, 1)
+    SY.wait_ge(sem.ycp, 1)
+    if not last and not first:
+        SY.wait_ge(sem.sent, 2 * out_engines)
+    SY.dma_start(T.y[:], T.ysb[:]).then_inc(sem.yst, 16)
+    SY.wait_ge(sem.yst, 16)

@@ -5,8 +5,7 @@ TW = 4 * NC
 G = 4
 C = 0.0259
 BANK = 512
-PIECES = ((0, 4), (4, 7), (7, 8))
-SEND_ENGINES = 8
+CODES, PLANE = "float8_e4m3fn_x4", "uint8"
 
 SCRATCH = {
     "sb": ("sbuf", [128, TW], "bfloat16"),
@@ -14,60 +13,107 @@ SCRATCH = {
     "wb": ("sbuf", [128, 2 * G * TW], "bfloat16"),
     "vb": ("sbuf", [128, TW], "bfloat16"),
     "h": ("sbuf", [128, TW], "bfloat16"),
-    "cqi": ("sbuf", [128, NC], "float8_e4m3fn_x4"), "pqi": ("sbuf", [128, NC], "uint8"),
-    "cx": ("sbuf", [128, NC], "float8_e4m3fn_x4"), "px": ("sbuf", [128, NC], "uint8"),
-    "cw": ("sbuf", [128, 2 * G * NC], "float8_e4m3fn_x4"), "pw": ("sbuf", [128, 2 * G * NC], "uint8"),
-    "cv": ("sbuf", [128, NC], "float8_e4m3fn_x4"), "pv": ("sbuf", [128, NC], "uint8"),
-    "cqo": ("sbuf", [128, NC], "float8_e4m3fn_x4"), "pqo": ("sbuf", [128, NC], "uint8"),
+    "cqi": ("sbuf", [128, NC], CODES), "pqi": ("sbuf", [128, NC], PLANE),
+    "cx": ("sbuf", [128, NC], CODES), "px": ("sbuf", [128, NC], PLANE),
+    "cw": ("sbuf", [128, 2 * G * NC], CODES), "pw": ("sbuf", [128, 2 * G * NC], PLANE),
+    "cqo": ("sbuf", [128, NC], CODES), "pqo": ("sbuf", [128, NC], PLANE),
+    "cxs": ("sbuf", [128, NC], CODES), "pxs": ("sbuf", [128, NC], PLANE),
+    "cws": ("sbuf", [128, 2 * G * NC], CODES), "pws": ("sbuf", [128, 2 * G * NC], PLANE),
+    "cv": ("sbuf", [128, NC], CODES), "pv": ("sbuf", [128, NC], PLANE),
+    "cqy": ("sbuf", [128, NC], CODES), "pqy": ("sbuf", [128, NC], PLANE),
     "ysb": ("sbuf", [128, NC], "float32"),
     "z": ("psum", [128, G * BANK], "float32"),
     "yp": ("psum", [128, BANK], "float32"),
 }
 SEMAPHORES = (["ls", "lx", "lv", "lw0", "lw1", "lw2"]
               + ["qs", "qx", "qv", "qw0", "qw1", "qw2", "qo"]
-              + ["mm0", "mm1", "mm2", "mm3", "acts", "ymm", "ycp", "yst"]
-              + ["arrived", "sent"])
+              + ["ax", "aw0", "aw1", "aw2", "arrived", "ay"]
+              + ["mm0", "mm1", "mm2", "mm3", "acts", "ymm", "ycp", "yst", "sent"])
 
 
 def hop_mask(topo, src, dst):
     allowed = topo.mask(src, dst)
-    engines = [e for e in range(allowed.bit_length()) if (allowed >> e) & 1]
-    chosen = engines[::max(1, len(engines) // SEND_ENGINES)]
-    return sum(1 << e for e in chosen), len(chosen)
+    return allowed, sum((allowed >> e) & 1 for e in range(allowed.bit_length()))
+
+
+def plan(cores, topo):
+    n = len(cores)
+    place = list(range(n))
+    for r in range(1, n - 2):
+        before, a, b = cores[place[r - 1]], cores[r], cores[r + 1]
+        if (topo.chip(a) != topo.chip(before) and topo.chip(b) == topo.chip(a)
+                and topo.die(a) != topo.die(before) and topo.die(b) == topo.die(before)):
+            place[r], place[r + 1] = r + 1, r
+    return place
 
 
 def rank_program(g, core, T, topo):
     rank = T.rank_of(core)
     if rank is None:
         return
-    n_ranks = len(T.cores)
-    first, last = rank == 0, rank == n_ranks - 1
+    cores = T.cores
+    n_ranks = len(cores)
+    place = plan(cores, topo)
+    layer = place.index(rank)
+    moved = layer != rank
+    first, last = layer == 0, layer == n_ranks - 1
     sem = T.sem
     TE, V, S, SY = g.tensor, g.vector, g.scalar, g.sync
+    pieces = ((0, 4), (4, 7), (7, 8)) if first else ((0, 4), (4, 8))
+
+    def engines(src, dst):
+        return hop_mask(topo, src, dst)[1]
+
+    outs = []
     if not last:
-        nxt = T.cores[rank + 1]
-        if not topo.may_write(core, nxt):
-            raise ValueError("no direct write from core %d to core %d" % (core, nxt))
-        out_mask, out_engines = hop_mask(topo, core, nxt)
+        outs.append((cores[place[layer + 1]], T.cqi, T.pqi, sem.arrived))
+    if moved and cores[layer] not in [o[0] for o in outs]:
+        outs.append((cores[layer], T.cqy, T.pqy, sem.ay))
+    keeper = cores[place[rank]]
+    all_sent = sum(2 * engines(core, o[0]) for o in outs) + (2 * (1 + len(pieces)) * engines(core, keeper) if moved else 0)
+
+    def send(dst, dst_codes, dst_plane, codes, plane, there):
+        if not topo.may_write(core, dst):
+            raise ValueError("no direct write from core %d to core %d" % (core, dst))
+        rid, pid, _ = topo.addr(dst)
+        mask = hop_mask(topo, core, dst)[0]
+        g.remote_dma(dst_codes.bitcast(dt.uint8), codes.bitcast(dt.uint8), there, sem.sent, pid, rid, mask)
+        g.remote_dma(dst_plane, plane, there, sem.sent, pid, rid, mask)
 
     if first:
         SY.dma_start(T.sb[:], T.s[:]).then_inc(sem.ls, 16)
     S.dma_start(T.xb[:], T.x[:]).then_inc(sem.lx, 16)
-    for j, (a, b) in enumerate(PIECES):
+    for j, (a, b) in enumerate(pieces):
         (S if j % 2 else SY).dma_start(T.wb[:, TW * a:TW * b], T.w[:, TW * a:TW * b]).then_inc(sem["lw%d" % j], 16)
     if first:
-        SY.wait_ge(sem.sent, 2 * out_engines)
-        SY.dma_start(T.vb[:], T.v[:]).then_inc(sem.lv, 16)
-    else:
-        S.dma_start(T.vb[:], T.v[:]).then_inc(sem.lv, 16)
+        SY.wait_ge(sem.sent, all_sent)
+    SY.dma_start(T.vb[:], T.v[:]).then_inc(sem.lv, 16)
+
+    own_cx, own_px, own_cw, own_pw = (T.cxs, T.pxs, T.cws, T.pws) if moved else (T.cx, T.px, T.cw, T.pw)
 
     def quantise(loaded, codes, plane, tile, done):
         V.wait_ge(loaded, 16)
         V.quantize_mx(codes, plane, tile).then_inc(done, 1)
 
+    def quantise_x():
+        quantise(sem.lx, own_cx[:], own_px[:], T.xb[:], sem.qx)
+        if moved:
+            g.wait_ge(sem.qx, 1)
+            send(keeper, T.cx[:], T.px[:], own_cx[:], own_px[:], sem.ax)
+
     def quantise_w(j):
-        a, b = PIECES[j]
-        quantise(sem["lw%d" % j], T.cw[:, NC * a:NC * b], T.pw[:, NC * a:NC * b], T.wb[:, TW * a:TW * b], sem["qw%d" % j])
+        a, b = pieces[j]
+        quantise(sem["lw%d" % j], own_cw[:, NC * a:NC * b], own_pw[:, NC * a:NC * b], T.wb[:, TW * a:TW * b], sem["qw%d" % j])
+        if moved:
+            g.wait_ge(sem["qw%d" % j], 1)
+            send(keeper, T.cw[:, NC * a:NC * b], T.pw[:, NC * a:NC * b], own_cw[:, NC * a:NC * b], own_pw[:, NC * a:NC * b],
+                 sem["aw%d" % j])
+
+    def have(what):
+        if moved:
+            TE.wait_ge(sem["a" + what], 2 * engines(cores[layer], core))
+        else:
+            TE.wait_ge(sem["q" + what], 1)
 
     def product(i, t, start, stop):
         k = 2 * i + t
@@ -84,64 +130,69 @@ def rank_program(g, core, T, topo):
             S.wait_ge(sem["mm%d" % b], 1)
             S.activation(out, z, ActivationFunctionType.Relu, scale=C).then_inc(sem.acts, 1)
 
-    piece_of = {k: j for j, (a, b) in enumerate(PIECES) for k in range(a, b)}
+    piece_of = {k: j for j, (a, b) in enumerate(pieces) for k in range(a, b)}
     if first:
         quantise(sem.ls, T.cqi[:], T.pqi[:], T.sb[:], sem.qs)
-        quantise(sem.lx, T.cx[:], T.px[:], T.xb[:], sem.qx)
+        quantise_x()
         quantise_w(0)
         act(1)
         quantise_w(1)
         quantise_w(2)
         TE.wait_ge(sem.qs, 1)
-        TE.wait_ge(sem.qx, 1)
+        have("x")
         seen = -1
         for i in range(G):
             for t in range(2):
                 if piece_of[2 * i + t] > seen:
                     seen = piece_of[2 * i + t]
-                    TE.wait_ge(sem["qw%d" % seen], 1)
+                    have("w%d" % seen)
                 p = product(i, t, t == 0, t == 1)
             p.then_inc(sem["mm%d" % i], 1)
         act(0)
         act(2)
         act(3)
     else:
-        quantise(sem.lx, T.cx[:], T.px[:], T.xb[:], sem.qx)
-        for j in range(len(PIECES)):
+        quantise_x()
+        for j in range(len(pieces)):
             quantise_w(j)
         quantise(sem.lv, T.cv[:], T.pv[:], T.vb[:], sem.qv)
-        TE.wait_ge(sem.qx, 1)
+        have("x")
         seen = -1
         for i in range(G):
             if piece_of[2 * i + 1] > seen:
-                for j in range(seen + 1, piece_of[2 * i + 1] + 1):
-                    TE.wait_ge(sem["qw%d" % j], 1)
                 seen = piece_of[2 * i + 1]
+                have("w%d" % seen)
             product(i, 1, True, False)
-        in_engines = hop_mask(topo, T.cores[rank - 1], core)[1]
-        TE.wait_ge(sem.arrived, 2 * in_engines)
+        TE.wait_ge(sem.arrived, 2 * engines(cores[place[layer - 1]], core))
         for i in range(G):
             product(i, 0, False, True).then_inc(sem["mm%d" % i], 1)
             act(i)
 
     V.wait_ge(sem.acts, G)
     V.quantize_mx(T.cqo[:], T.pqo[:], T.h[:]).then_inc(sem.qo, 1)
-    if not last:
-        rid, pid, _ = topo.addr(nxt)
+    if outs:
         g.wait_ge(sem.qo, 1)
-        g.remote_dma(T.cqi[:].bitcast(dt.uint8), T.cqo[:].bitcast(dt.uint8), sem.arrived, sem.sent, pid, rid, out_mask)
-        g.remote_dma(T.pqi[:], T.pqo[:], sem.arrived, sem.sent, pid, rid, out_mask)
-        g.wait_ge(sem.sent, 2 * out_engines)
+        for dst, codes, plane, there in outs:
+            send(dst, codes[:], plane[:], T.cqo[:], T.pqo[:], there)
+    if all_sent:
+        g.wait_ge(sem.sent, all_sent)
 
     if first:
         quantise(sem.lv, T.cv[:], T.pv[:], T.vb[:], sem.qv)
     TE.wait_ge(sem.qv, 1)
-    TE.wait_ge(sem.qo, 1)
-    TE.matmul_mx(T.yp[:, 0:NC], T.cv[:], T.pv[:], T.cqo[:], T.pqo[:], True, True).then_inc(sem.ymm, 1)
+    if not moved:
+        TE.wait_ge(sem.qo, 1)
+        yc, yq = T.cqo, T.pqo
+    elif layer == rank + 1:
+        yc, yq = T.cqi, T.pqi
+    else:
+        TE.wait_ge(sem.ay, 2 * engines(keeper, core))
+        yc, yq = T.cqy, T.pqy
+    TE.matmul_mx(T.yp[:, 0:NC], T.cv[:], T.pv[:], yc[:], yq[:], True, True).then_inc(sem.ymm, 1)
     V.wait_ge(sem.ymm, 1)
     V.tensor_copy(T.ysb[:], T.yp[:, 0:NC]).then_inc(sem.ycp, 1)
     SY.wait_ge(sem.ycp, 1)
-    if not last and not first:
-        SY.wait_ge(sem.sent, 2 * out_engines)
+    if all_sent and not first:
+        SY.wait_ge(sem.sent, all_sent)
     SY.dma_start(T.y[:], T.ysb[:]).then_inc(sem.yst, 16)
     SY.wait_ge(sem.yst, 16)

@@ -39,11 +39,13 @@ def hop_mask(topo, src, dst):
 def plan(cores, topo):
     n = len(cores)
     place = list(range(n))
-    for r in range(1, n - 2):
-        before, a, b = cores[place[r - 1]], cores[r], cores[r + 1]
-        if (topo.chip(a) != topo.chip(before) and topo.chip(b) == topo.chip(a)
-                and topo.die(a) != topo.die(before) and topo.die(b) == topo.die(before)):
+    r = 1
+    while r < n - 2:
+        if topo.chip(cores[r]) == topo.chip(cores[r + 1]) and topo.chip(cores[r]) != topo.chip(cores[0]):
             place[r], place[r + 1] = r + 1, r
+            r += 2
+        else:
+            r += 1
     return place
 
 
@@ -87,7 +89,9 @@ def rank_program(g, core, T, topo):
         (S if j % 2 else SY).dma_start(T.wb[:, TW * a:TW * b], T.w[:, TW * a:TW * b]).then_inc(sem["lw%d" % j], 16)
     if first:
         SY.wait_ge(sem.sent, all_sent)
-    SY.dma_start(T.vb[:], T.v[:]).then_inc(sem.lv, 16)
+        SY.dma_start(T.vb[:], T.v[:]).then_inc(sem.lv, 16)
+    else:
+        S.dma_start(T.vb[:], T.v[:]).then_inc(sem.lv, 16)
 
     own_cx, own_px, own_cw, own_pw = (T.cxs, T.pxs, T.cws, T.pws) if moved else (T.cx, T.px, T.cw, T.pw)
 

@@ -6,6 +6,8 @@ G = 4
 C = 0.0259
 BANK = 512
 CODES, PLANE = "float8_e4m3fn_x4", "uint8"
+HEAD = ((0, 2), (2, 4), (4, 6), (6, 7), (7, 8))
+BODY = ((0, 4), (4, 8))
 
 SCRATCH = {
     "sb": ("sbuf", [128, TW], "bfloat16"),
@@ -25,15 +27,18 @@ SCRATCH = {
     "z": ("psum", [128, G * BANK], "float32"),
     "yp": ("psum", [128, BANK], "float32"),
 }
-SEMAPHORES = (["ls", "lx", "lv", "lw0", "lw1", "lw2"]
-              + ["qs", "qx", "qv", "qw0", "qw1", "qw2", "qo"]
-              + ["ax", "aw0", "aw1", "aw2", "arrived", "ay"]
+SEMAPHORES = (["ls", "lx", "lv"] + ["lw%d" % j for j in range(len(HEAD))]
+              + ["qs", "qx", "qv", "qo"] + ["qw%d" % j for j in range(len(HEAD))]
+              + ["ax", "arrived", "ay"] + ["aw%d" % j for j in range(len(BODY))]
               + ["mm0", "mm1", "mm2", "mm3", "acts", "ymm", "ycp", "yst", "sent"])
 
 
-def hop_mask(topo, src, dst):
-    allowed = topo.mask(src, dst)
-    return allowed, sum((allowed >> e) & 1 for e in range(allowed.bit_length()))
+def bits(mask):
+    return [e for e in range(mask.bit_length()) if (mask >> e) & 1]
+
+
+def count(mask):
+    return len(bits(mask))
 
 
 def plan(cores, topo):
@@ -61,26 +66,50 @@ def rank_program(g, core, T, topo):
     first, last = layer == 0, layer == n_ranks - 1
     sem = T.sem
     TE, V, S, SY = g.tensor, g.vector, g.scalar, g.sync
-    pieces = ((0, 4), (4, 7), (7, 8)) if first else ((0, 4), (4, 8))
+    pieces = HEAD if first else BODY
 
-    def engines(src, dst):
-        return hop_mask(topo, src, dst)[1]
+    def bringer(l):
+        if place[l] == l or place[l + 1] == l:
+            return None
+        if place[l + 1] == l + 1 and l + 1 < n_ranks - 1:
+            return l + 1
+        return place[l]
+
+    def ship_mask(r):
+        return topo.mask(cores[r], cores[place[r]]) if place[r] != r else 0
+
+    def pass_mask(r):
+        return topo.mask(cores[r], cores[r - 1]) if r > 0 and place[r] == r and bringer(r - 1) == r else 0
+
+    def q_masks(r, dst):
+        allowed = topo.mask(cores[r], dst)
+        if ship_mask(r):
+            return allowed, allowed
+        if pass_mask(r) and allowed & ~pass_mask(r) and allowed & pass_mask(r):
+            return allowed & ~pass_mask(r), allowed & pass_mask(r)
+        if topo.chip(cores[r]) == topo.chip(dst):
+            e = bits(allowed)
+            return sum(1 << k for k in e[0::2]), sum(1 << k for k in e[1::2])
+        return allowed, allowed
+
+    def q_count(r, dst):
+        return sum(count(m) for m in q_masks(r, dst))
 
     outs = []
     if not last:
         outs.append((cores[place[layer + 1]], T.cqi, T.pqi, sem.arrived))
-    if moved and cores[layer] not in [o[0] for o in outs]:
-        outs.append((cores[layer], T.cqy, T.pqy, sem.ay))
+        if bringer(layer) == rank:
+            outs.append((cores[layer], T.cqy, T.pqy, sem.ay))
     keeper = cores[place[rank]]
-    all_sent = sum(2 * engines(core, o[0]) for o in outs) + (2 * (1 + len(pieces)) * engines(core, keeper) if moved else 0)
+    all_sent = (sum(q_count(rank, o[0]) for o in outs) + 2 * (1 + len(pieces)) * count(ship_mask(rank))
+                + 2 * count(pass_mask(rank)))
 
-    def send(dst, dst_codes, dst_plane, codes, plane, there):
+    def send(dst, masks, dst_codes, dst_plane, codes, plane, there):
         if not topo.may_write(core, dst):
             raise ValueError("no direct write from core %d to core %d" % (core, dst))
         rid, pid, _ = topo.addr(dst)
-        mask = hop_mask(topo, core, dst)[0]
-        g.remote_dma(dst_codes.bitcast(dt.uint8), codes.bitcast(dt.uint8), there, sem.sent, pid, rid, mask)
-        g.remote_dma(dst_plane, plane, there, sem.sent, pid, rid, mask)
+        g.remote_dma(dst_codes.bitcast(dt.uint8), codes.bitcast(dt.uint8), there, sem.sent, pid, rid, masks[0])
+        g.remote_dma(dst_plane, plane, there, sem.sent, pid, rid, masks[1])
 
     if first:
         SY.dma_start(T.sb[:], T.s[:]).then_inc(sem.ls, 16)
@@ -94,6 +123,7 @@ def rank_program(g, core, T, topo):
         S.dma_start(T.vb[:], T.v[:]).then_inc(sem.lv, 16)
 
     own_cx, own_px, own_cw, own_pw = (T.cxs, T.pxs, T.cws, T.pws) if moved else (T.cx, T.px, T.cw, T.pw)
+    ship = (ship_mask(rank), ship_mask(rank))
 
     def quantise(loaded, codes, plane, tile, done):
         V.wait_ge(loaded, 16)
@@ -103,19 +133,19 @@ def rank_program(g, core, T, topo):
         quantise(sem.lx, own_cx[:], own_px[:], T.xb[:], sem.qx)
         if moved:
             g.wait_ge(sem.qx, 1)
-            send(keeper, T.cx[:], T.px[:], own_cx[:], own_px[:], sem.ax)
+            send(keeper, ship, T.cx[:], T.px[:], own_cx[:], own_px[:], sem.ax)
 
     def quantise_w(j):
         a, b = pieces[j]
         quantise(sem["lw%d" % j], own_cw[:, NC * a:NC * b], own_pw[:, NC * a:NC * b], T.wb[:, TW * a:TW * b], sem["qw%d" % j])
         if moved:
             g.wait_ge(sem["qw%d" % j], 1)
-            send(keeper, T.cw[:, NC * a:NC * b], T.pw[:, NC * a:NC * b], own_cw[:, NC * a:NC * b], own_pw[:, NC * a:NC * b],
-                 sem["aw%d" % j])
+            send(keeper, ship, T.cw[:, NC * a:NC * b], T.pw[:, NC * a:NC * b], own_cw[:, NC * a:NC * b],
+                 own_pw[:, NC * a:NC * b], sem["aw%d" % j])
 
     def have(what):
         if moved:
-            TE.wait_ge(sem["a" + what], 2 * engines(cores[layer], core))
+            TE.wait_ge(sem["a" + what], 2 * count(ship_mask(layer)))
         else:
             TE.wait_ge(sem["q" + what], 1)
 
@@ -125,9 +155,9 @@ def rank_program(g, core, T, topo):
         return TE.matmul_mx(T.z[:, BANK * i:BANK * i + NC], T.cw[:, NC * k:NC * k + NC], T.pw[:, NC * k:NC * k + NC],
                             rhs[:], rhs_scale[:], start, stop)
 
-    def act(b):
+    def act(b, on_vector):
         out, z = T.h[:, b:TW:G], T.z[:, BANK * b:BANK * b + NC]
-        if b % 2:
+        if on_vector:
             V.wait_ge(sem["mm%d" % b], 1)
             V.tensor_scalar(out, z, 0.0, C, AluOpType.max, AluOpType.mult).then_inc(sem.acts, 1)
         else:
@@ -138,10 +168,8 @@ def rank_program(g, core, T, topo):
     if first:
         quantise(sem.ls, T.cqi[:], T.pqi[:], T.sb[:], sem.qs)
         quantise_x()
-        quantise_w(0)
-        act(1)
-        quantise_w(1)
-        quantise_w(2)
+        for j in range(len(pieces)):
+            quantise_w(j)
         TE.wait_ge(sem.qs, 1)
         have("x")
         seen = -1
@@ -152,9 +180,7 @@ def rank_program(g, core, T, topo):
                     have("w%d" % seen)
                 p = product(i, t, t == 0, t == 1)
             p.then_inc(sem["mm%d" % i], 1)
-        act(0)
-        act(2)
-        act(3)
+            act(i, i == G - 1)
     else:
         quantise_x()
         for j in range(len(pieces)):
@@ -167,17 +193,21 @@ def rank_program(g, core, T, topo):
                 seen = piece_of[2 * i + 1]
                 have("w%d" % seen)
             product(i, 1, True, False)
-        TE.wait_ge(sem.arrived, 2 * engines(cores[place[layer - 1]], core))
+        landed = q_count(place[layer - 1], core)
+        TE.wait_ge(sem.arrived, landed)
         for i in range(G):
             product(i, 0, False, True).then_inc(sem["mm%d" % i], 1)
-            act(i)
+            act(i, i % 2 == 1)
+        if pass_mask(rank):
+            g.wait_ge(sem.arrived, landed)
+            send(cores[rank - 1], (pass_mask(rank), pass_mask(rank)), T.cqy[:], T.pqy[:], T.cqi[:], T.pqi[:], sem.ay)
 
     V.wait_ge(sem.acts, G)
     V.quantize_mx(T.cqo[:], T.pqo[:], T.h[:]).then_inc(sem.qo, 1)
     if outs:
         g.wait_ge(sem.qo, 1)
         for dst, codes, plane, there in outs:
-            send(dst, codes[:], plane[:], T.cqo[:], T.pqo[:], there)
+            send(dst, q_masks(rank, dst), codes[:], plane[:], T.cqo[:], T.pqo[:], there)
     if all_sent:
         g.wait_ge(sem.sent, all_sent)
 
@@ -190,7 +220,8 @@ def rank_program(g, core, T, topo):
     elif layer == rank + 1:
         yc, yq = T.cqi, T.pqi
     else:
-        TE.wait_ge(sem.ay, 2 * engines(keeper, core))
+        by = bringer(rank)
+        TE.wait_ge(sem.ay, q_count(by, core) if by == place[rank] else 2 * count(pass_mask(by)))
         yc, yq = T.cqy, T.pqy
     TE.matmul_mx(T.yp[:, 0:NC], T.cv[:], T.pv[:], yc[:], yq[:], True, True).then_inc(sem.ymm, 1)
     V.wait_ge(sem.ymm, 1)

from concourse.mybir import dt, AluOpType, ActivationFunctionType

NC = 128
TW = 4 * NC
G = 4
C = 0.0259
BANK = 512
CODES, PLANE = "float8_e4m3fn_x4", "uint8"
HEAD = ((0, 2), (2, 4), (4, 6), (6, 7), (7, 8))
BODY = ((0, 4), (4, 8))

SCRATCH = {
    "sb": ("sbuf", [128, TW], "bfloat16"),
    "xb": ("sbuf", [128, TW], "bfloat16"),
    "wb": ("sbuf", [128, 2 * G * TW], "bfloat16"),
    "vb": ("sbuf", [128, TW], "bfloat16"),
    "h": ("sbuf", [128, TW], "bfloat16"),
    "cqi": ("sbuf", [128, NC], CODES), "pqi": ("sbuf", [128, NC], PLANE),
    "cx": ("sbuf", [128, NC], CODES), "px": ("sbuf", [128, NC], PLANE),
    "cw": ("sbuf", [128, 2 * G * NC], CODES), "pw": ("sbuf", [128, 2 * G * NC], PLANE),
    "cqo": ("sbuf", [128, NC], CODES), "pqo": ("sbuf", [128, NC], PLANE),
    "cxs": ("sbuf", [128, NC], CODES), "pxs": ("sbuf", [128, NC], PLANE),
    "cws": ("sbuf", [128, 2 * G * NC], CODES), "pws": ("sbuf", [128, 2 * G * NC], PLANE),
    "cv": ("sbuf", [128, NC], CODES), "pv": ("sbuf", [128, NC], PLANE),
    "cqy": ("sbuf", [128, NC], CODES), "pqy": ("sbuf", [128, NC], PLANE),
    "ysb": ("sbuf", [128, NC], "float32"),
    "z": ("psum", [128, G * BANK], "float32"),
    "yp": ("psum", [128, BANK], "float32"),
}
SEMAPHORES = (["ls", "lx", "lv"] + ["lw%d" % j for j in range(len(HEAD))]
              + ["qs", "qx", "qv", "qo"] + ["qw%d" % j for j in range(len(HEAD))]
              + ["ax", "arrived", "ay"] + ["aw%d" % j for j in range(len(BODY))]
              + ["mm0", "mm1", "mm2", "mm3", "acts", "ymm", "ycp", "yst", "sent"])


def bits(mask):
    return [e for e in range(mask.bit_length()) if (mask >> e) & 1]


def count(mask):
    return len(bits(mask))


def plan(cores, topo):
    n = len(cores)
    place = list(range(n))
    r = 1
    while r < n - 2:
        if topo.chip(cores[r]) == topo.chip(cores[r + 1]) and topo.chip(cores[r]) != topo.chip(cores[0]):
            place[r], place[r + 1] = r + 1, r
            r += 2
        else:
            r += 1
    return place


def rank_program(g, core, T, topo):
    rank = T.rank_of(core)
    if rank is None:
        return
    cores = T.cores
    n_ranks = len(cores)
    place = plan(cores, topo)
    layer = place.index(rank)
    moved = layer != rank
    first, last = layer == 0, layer == n_ranks - 1
    sem = T.sem
    TE, V, S, SY = g.tensor, g.vector, g.scalar, g.sync
    pieces = HEAD if first else BODY

    def bringer(l):
        if place[l] == l or place[l + 1] == l:
            return None
        if place[l + 1] == l + 1 and l + 1 < n_ranks - 1:
            return l + 1
        return place[l]

    def ship_mask(r):
        return topo.mask(cores[r], cores[place[r]]) if place[r] != r else 0

    def pass_mask(r):
        return topo.mask(cores[r], cores[r - 1]) if r > 0 and place[r] == r and bringer(r - 1) == r else 0

    def q_masks(r, dst):
        allowed = topo.mask(cores[r], dst)
        if ship_mask(r):
            return allowed, allowed
        if pass_mask(r) and allowed & ~pass_mask(r) and allowed & pass_mask(r):
            return allowed & ~pass_mask(r), allowed & pass_mask(r)
        if topo.chip(cores[r]) == topo.chip(dst):
            e = bits(allowed)
            return sum(1 << k for k in e[0::2]), sum(1 << k for k in e[1::2])
        return allowed, allowed

    def q_count(r, dst):
        return sum(count(m) for m in q_masks(r, dst))

    outs = []
    if not last:
        outs.append((cores[place[layer + 1]], T.cqi, T.pqi, sem.arrived))
        if bringer(layer) == rank:
            outs.append((cores[layer], T.cqy, T.pqy, sem.ay))
    keeper = cores[place[rank]]
    all_sent = (sum(q_count(rank, o[0]) for o in outs) + 2 * (1 + len(pieces)) * count(ship_mask(rank))
                + 2 * count(pass_mask(rank)))

    def send(dst, masks, dst_codes, dst_plane, codes, plane, there):
        if not topo.may_write(core, dst):
            raise ValueError("no direct write from core %d to core %d" % (core, dst))
        rid, pid, _ = topo.addr(dst)
        g.remote_dma(dst_codes.bitcast(dt.uint8), codes.bitcast(dt.uint8), there, sem.sent, pid, rid, masks[0])
        g.remote_dma(dst_plane, plane, there, sem.sent, pid, rid, masks[1])

    if first:
        SY.dma_start(T.sb[:], T.s[:]).then_inc(sem.ls, 16)
    S.dma_start(T.xb[:], T.x[:]).then_inc(sem.lx, 16)
    for j, (a, b) in enumerate(pieces):
        (S if j % 2 else SY).dma_start(T.wb[:, TW * a:TW * b], T.w[:, TW * a:TW * b]).then_inc(sem["lw%d" % j], 16)
    if first:
        SY.wait_ge(sem.sent, all_sent)
        SY.dma_start(T.vb[:], T.v[:]).then_inc(sem.lv, 16)
    else:
        S.dma_start(T.vb[:], T.v[:]).then_inc(sem.lv, 16)

    own_cx, own_px, own_cw, own_pw = (T.cxs, T.pxs, T.cws, T.pws) if moved else (T.cx, T.px, T.cw, T.pw)
    ship = (ship_mask(rank), ship_mask(rank))

    def quantise(loaded, codes, plane, tile, done):
        V.wait_ge(loaded, 16)
        V.quantize_mx(codes, plane, tile).then_inc(done, 1)

    def quantise_x():
        quantise(sem.lx, own_cx[:], own_px[:], T.xb[:], sem.qx)
        if moved:
            g.wait_ge(sem.qx, 1)
            send(keeper, ship, T.cx[:], T.px[:], own_cx[:], own_px[:], sem.ax)

    def quantise_w(j):
        a, b = pieces[j]
        quantise(sem["lw%d" % j], own_cw[:, NC * a:NC * b], own_pw[:, NC * a:NC * b], T.wb[:, TW * a:TW * b], sem["qw%d" % j])
        if moved:
            g.wait_ge(sem["qw%d" % j], 1)
            send(keeper, ship, T.cw[:, NC * a:NC * b], T.pw[:, NC * a:NC * b], own_cw[:, NC * a:NC * b],
                 own_pw[:, NC * a:NC * b], sem["aw%d" % j])

    def have(what):
        if moved:
            TE.wait_ge(sem["a" + what], 2 * count(ship_mask(layer)))
        else:
            TE.wait_ge(sem["q" + what], 1)

    def product(i, t, start, stop):
        k = 2 * i + t
        rhs, rhs_scale = (T.cqi, T.pqi) if t == 0 else (T.cx, T.px)
        return TE.matmul_mx(T.z[:, BANK * i:BANK * i + NC], T.cw[:, NC * k:NC * k + NC], T.pw[:, NC * k:NC * k + NC],
                            rhs[:], rhs_scale[:], start, stop)

    def act(b, on_vector):
        out, z = T.h[:, b:TW:G], T.z[:, BANK * b:BANK * b + NC]
        if on_vector:
            V.wait_ge(sem["mm%d" % b], 1)
            V.tensor_scalar(out, z, 0.0, C, AluOpType.max, AluOpType.mult).then_inc(sem.acts, 1)
        else:
            S.wait_ge(sem["mm%d" % b], 1)
            S.activation(out, z, ActivationFunctionType.Relu, scale=C).then_inc(sem.acts, 1)

    piece_of = {k: j for j, (a, b) in enumerate(pieces) for k in range(a, b)}
    if first:
        quantise(sem.ls, T.cqi[:], T.pqi[:], T.sb[:], sem.qs)
        quantise_x()
        for j in range(len(pieces)):
            quantise_w(j)
        TE.wait_ge(sem.qs, 1)
        have("x")
        seen = -1
        for i in range(G):
            for t in range(2):
                if piece_of[2 * i + t] > seen:
                    seen = piece_of[2 * i + t]
                    have("w%d" % seen)
                p = product(i, t, t == 0, t == 1)
            p.then_inc(sem["mm%d" % i], 1)
            act(i, i == G - 1)
    else:
        quantise_x()
        for j in range(len(pieces)):
            quantise_w(j)
        quantise(sem.lv, T.cv[:], T.pv[:], T.vb[:], sem.qv)
        have("x")
        seen = -1
        for i in range(G):
            if piece_of[2 * i + 1] > seen:
                seen = piece_of[2 * i + 1]
                have("w%d" % seen)
            product(i, 1, True, False)
        landed = q_count(place[layer - 1], core)
        TE.wait_ge(sem.arrived, landed)
        for i in range(G):
            product(i, 0, False, True).then_inc(sem["mm%d" % i], 1)
            act(i, i % 2 == 1)
        if pass_mask(rank):
            g.wait_ge(sem.arrived, landed)
            send(cores[rank - 1], (pass_mask(rank), pass_mask(rank)), T.cqy[:], T.pqy[:], T.cqi[:], T.pqi[:], sem.ay)

    V.wait_ge(sem.acts, G)
    V.quantize_mx(T.cqo[:], T.pqo[:], T.h[:]).then_inc(sem.qo, 1)
    if outs:
        g.wait_ge(sem.qo, 1)
        for dst, codes, plane, there in outs:
            send(dst, q_masks(rank, dst), codes[:], plane[:], T.cqo[:], T.pqo[:], there)
    if all_sent:
        g.wait_ge(sem.sent, all_sent)

    if first:
        quantise(sem.lv, T.cv[:], T.pv[:], T.vb[:], sem.qv)
    TE.wait_ge(sem.qv, 1)
    if not moved:
        TE.wait_ge(sem.qo, 1)
        yc, yq = T.cqo, T.pqo
    elif layer == rank + 1:
        yc, yq = T.cqi, T.pqi
    else:
        by = bringer(rank)
        TE.wait_ge(sem.ay, q_count(by, core) if by == place[rank] else 2 * count(pass_mask(by)))
        yc, yq = T.cqy, T.pqy
    TE.matmul_mx(T.yp[:, 0:NC], T.cv[:], T.pv[:], yc[:], yq[:], True, True).then_inc(sem.ymm, 1)
    V.wait_ge(sem.ymm, 1)
    V.tensor_copy(T.ysb[:], T.yp[:, 0:NC]).then_inc(sem.ycp, 1)
    SY.wait_ge(sem.ycp, 1)
    if all_sent and not first:
        SY.wait_ge(sem.sent, all_sent)
    SY.dma_start(T.y[:], T.ysb[:]).then_inc(sem.yst, 16)
    SY.wait_ge(sem.yst, 16)
